import numpy as np
import ml_dtypes


def mxq(x, axis, fmt="e4m3"):
    dtype, down = {"e4m3": (ml_dtypes.float8_e4m3fn, 7), "e5m2": (ml_dtypes.float8_e5m2, 14)}[fmt]
    v = np.moveaxis(np.asarray(x, np.float32).astype(ml_dtypes.bfloat16).astype(np.float64), axis, -1)
    blocks = v.reshape(v.shape[:-1] + (-1, 32))
    amax = np.abs(blocks).max(-1, keepdims=True)
    byte = np.maximum(np.where(amax > 0, np.frexp(amax)[1] - 1 + 127, 0) - down, 1)
    scale = np.exp2(byte - 127.0)
    codes = (blocks / scale).astype(np.float32).astype(dtype).astype(np.float64)
    return np.moveaxis((codes * scale).reshape(v.shape), -1, axis)


WIDE = False


def mx_kscale(k):
    if not WIDE:
        return np.ones(k)
    levels = np.array([10, -10, 5, -5, 0])
    if k % 512:
        return np.exp2(np.random.permutation(np.resize(levels, k // 32))).repeat(32)
    a = np.empty((k // 512, 16))
    for p in range(k // 512):
        a[p, :8] = np.random.permutation(np.resize(levels, 8))
        for g in range(8):
            far = levels[np.abs(levels - a[p, g]) >= 10]
            a[p, g + 8] = far[np.random.randint(len(far))]
    return np.exp2(a.ravel()).repeat(32)


def f64(x):
    return np.asarray(x).astype(np.float64)


def striped(idx):
    return np.tile(idx.reshape(-1, 16).T, (8, 1)).astype(np.uint16)


def unstriped(offs):
    return offs[:16].T.reshape(-1).astype(np.int64)


E2M1 = np.array([0.0, 0.5, 1.0, 1.5, 2.0, 3.0, 4.0, 6.0, -0.0, -0.5, -1.0, -1.5, -2.0, -3.0, -4.0, -6.0])


def pack_weight(w, fmt):
    k, n = w.shape
    w = f64(np.asarray(w, np.float32).astype(ml_dtypes.bfloat16)).reshape(k // 32, 32, n)
    amax = np.abs(w).max(1)
    if fmt == "e4m3":
        byte = np.frexp(amax)[1] - 1 + 127 - 7
    else:
        mant, ex = np.frexp(amax / 6.0)
        byte = np.where(mant > 0.5, ex, ex - 1) + 127
    byte = np.clip(np.where(amax > 0, byte, 1), 1, 254)
    scaled = (w * np.exp2(127.0 - byte)[:, None, :]).reshape(k, n).astype(np.float32)
    by_word = np.ascontiguousarray(scaled.reshape(k // 512, 128, 4, n).transpose(0, 1, 3, 2))
    if fmt == "e4m3":
        words = by_word.astype(ml_dtypes.float8_e4m3fn).view(np.uint8)
    else:
        c = by_word.astype(ml_dtypes.float4_e2m1fn).view(np.uint8) & 0xF
        words = (c[..., 0::2] | (c[..., 1::2] << 4)).reshape(k // 512, 128, 2 * n)
    return np.ascontiguousarray(words), np.ascontiguousarray(byte.astype(np.uint8).reshape(k // 512, 16, n))


def unpack_weight(words, scales, fmt):
    g, _, n = scales.shape
    words = np.ascontiguousarray(words).reshape(g, 128, n, -1)
    if fmt == "e4m3":
        vals = words.view(ml_dtypes.float8_e4m3fn).astype(np.float64)
    else:
        nib = np.empty((g, 128, n, 4), np.uint8)
        nib[..., 0::2] = words & 0xF
        nib[..., 1::2] = words >> 4
        vals = E2M1[nib]
    vals = vals * np.repeat(np.exp2(scales.astype(np.float64) - 127.0), 8, axis=1)[..., None]
    return vals.transpose(0, 1, 3, 2).reshape(g * 512, n)


def silu(v):
    return v / (1.0 + np.exp(-np.maximum(v, -700.0)))


K, T, E, C, F, D, H = 1024, 1024, 16, 128, 4, 128, 512
N = 128


def by_expert(wq, xq, E, C):
    return np.concatenate([wq[e].T @ xq[:, e * C:(e + 1) * C] for e in range(E)], axis=1)


def setup_inputs():
    n = np.random.standard_normal
    s = mx_kscale(K)
    u = mx_kscale(H)
    first = np.random.permutation(np.repeat(np.arange(E), T // E))
    second = (first + 1 + np.random.permutation(np.repeat(np.arange(E - 1), -(-T // (E - 1)))[:T])) % E
    while np.bincount(second, minlength=E).max() != T // E:
        load = np.bincount(second, minlength=E); hi, lo = int(load.argmax()), int(load.argmin())
        t = np.flatnonzero((second == hi) & (first != lo))[0]; second[t] = lo
    slot_token = np.empty(E * C, np.int64); pos = np.empty((2, T), np.int64); fill = np.zeros(E, np.int64)
    place = np.stack([np.random.permutation(C) for _ in range(E)])
    for r, deal in enumerate((first, second)):
        for t in np.random.permutation(T):
            e = deal[t]; j = e * C + place[e, fill[e]]; fill[e] += 1; slot_token[j] = t; pos[r, t] = j
    g = np.random.uniform(0.2, 0.8, T)
    slots2 = np.random.permutation(T)[:F * D]
    x = pack_weight(n((K, T)) * s[:, None], "e4m3")
    w = [pack_weight(m, "e2m1") for m in n((E, K, N)) / np.sqrt(K) / s[None, :, None]]
    return {
        "x_words": x[0],
        "x_scales": x[1],
        "w_words": np.stack([m[0] for m in w]),
        "w_scales": np.stack([m[1] for m in w]),
        "wa": (n((F, K, H)) / np.sqrt(K) / s[None, :, None] * u).astype(np.float32),
        "wb": (n((F, H, N)) / np.sqrt(H) / u[None, :, None]).astype(np.float32),
        "gate": np.stack([np.tile(g, (128, 1)), np.tile(1.0 - g, (128, 1))]).astype(np.float32),
        "gate2": (np.tile(np.random.uniform(0.2, 1.0, F * D), (128, 1))).astype(np.float32),
        "offs": striped(slot_token),
        "pos1": striped(pos[0]),
        "pos2": striped(pos[1]),
        "offs2": striped(slots2),
    }


def reference(x_words, x_scales, w_words, w_scales, wa, wb, gate, gate2, offs, pos1, pos2, offs2):
    w = np.stack([unpack_weight(w_words[e], w_scales[e], "e2m1") for e in range(E)])
    waq = mxq(f64(wa), 1, "e4m3")
    wbq = mxq(f64(wb), 1, "e4m3")
    idx, idx2 = unstriped(offs), unstriped(offs2)
    x = unpack_weight(x_words, x_scales, "e4m3")
    y = by_expert(w, x[:, idx], E, C)
    h = silu(by_expert(waq, x[:, idx2], F, D))
    z = by_expert(wbq, mxq(h, 0, "e4m3"), F, D)
    out = sum(f64(gate[r, :1]) * y[:, unstriped(p)] for r, p in enumerate((pos1, pos2)))
    out[:, idx2] += f64(gate2[:1]) * z
    return out

@@ -1,0 +1,251 @@
+from contextlib import ExitStack
+
+import concourse.mybir as mybir
+
+K, T, E, C, F, D, H, N = 1024, 1024, 16, 128, 4, 128, 512, 128
+FLOPS = 2 * K * N * E * C + 2 * K * H * F * D + 2 * H * N * F * D
+
+F32 = mybir.dt.float32
+BF16 = mybir.dt.bfloat16
+I32 = mybir.dt.int32
+U32 = mybir.dt.uint32
+U16 = mybir.dt.uint16
+U8 = mybir.dt.uint8
+FP8X4 = mybir.dt.float8_e4m3fn_x4
+FP4X4 = mybir.dt.float4_e2m1fn_x4
+MULT = mybir.AluOpType.mult
+ADD = mybir.AluOpType.add
+SILU = mybir.ActivationFunctionType.Silu
+
+P = 128
+PACK = 4
+PASS = P * PACK
+PASSES = K // PASS
+SLOTS = E * C
+BANK = 512
+CHUNKS = SLOTS // BANK
+PER_COL = 16
+
+
+def tile_moe_mlr_silu_kernel(
+    tc, x_words, x_scales, w_words, w_scales, wa, wb, gate, gate2, offs, pos1, pos2, offs2, out
+):
+    nc = tc.nc
+    with ExitStack() as ctx:
+        keep = ctx.enter_context(tc.tile_pool(name="keep", bufs=1))
+        psum = ctx.enter_context(tc.psum_pool(name="psum", bufs=1))
+
+        def sb(name, shape, dtype, tag=""):
+            return keep.tile(shape, dtype, name=name, align_bytes=64, tag=tag)
+
+        offs_sb = sb("offs_sb", [P, SLOTS // PER_COL], U16)
+        offs2_sb = sb("offs2_sb", [P, F * D // PER_COL], U16)
+        pos_sb = [sb("pos%d_sb" % r, [P, T // PER_COL], U16) for r in range(2)]
+        xs = sb("xs", [P, T], U8)
+        xw = [sb("xw%d" % s, [P, T], I32) for s in range(PASSES)]
+        ww = sb("ww", [P, E * PASSES, 2 * N], U8)
+        ws = sb("ws", [P, E * PASSES, N], U8)
+        es = [sb("es%d" % s, [P, SLOTS], U8) for s in range(PASSES)]
+        scattered = sb("scattered", [P, T], F32)
+        pieces = {(f, s): (2 if (f, s) in ((0, 0), (F - 1, PASSES - 1)) else 1) for f in range(F) for s in range(PASSES)}
+        wa_raw = {
+            (f, s): [sb("wa_raw%d%d%d" % (f, s, u), [P, PACK, H // n], F32) for u in range(n)] for (f, s), n in pieces.items()
+        }
+        wb_raw = sb("wb_raw", [P, F, PACK, N], F32)
+        g_sb = [sb("g%d" % r, [P, T], F32) for r in range(2)]
+        q_sb = sb("q_sb", [P, F * D], F32)
+
+        nc.vector.memset(xs[:].bitcast(I32), 0)
+        nc.vector.memset(ws[:].rearrange("p a n -> p (a n)").bitcast(I32), 0)
+        nc.vector.memset(es[1][:].bitcast(I32), 0)
+        nc.vector.memset(scattered[:], 0.0)
+
+        def load_wa(f, s):
+            width = H // pieces[f, s]
+            for u, raw in enumerate(wa_raw[f, s]):
+                src = wa[f, s * PASS : (s + 1) * PASS, u * width : (u + 1) * width]
+                nc.sync.dma_start(raw[:], src.rearrange("(p j) c -> p j c", j=PACK))
+
+        def load_xw(s):
+            nc.sync.dma_start(xw[s][:], x_words[s].rearrange("p t d -> p (t d)").bitcast(I32))
+
+        nc.sync.dma_start(offs_sb[:], offs)
+        nc.sync.dma_start(offs2_sb[:], offs2)
+        for q in range(4):
+            nc.sync.dma_start(xs[32 * q : 32 * q + 8, :].bitcast(I32), x_scales[:, 4 * q : 4 * q + 4, :].bitcast(I32))
+        load_wa(0, 0)
+        load_xw(0)
+        load_wa(0, 1)
+        load_xw(1)
+        load_wa(1, 0)
+        load_wa(1, 1)
+        load_wa(2, 0)
+        for q in range(4):
+            nc.sync.dma_start(
+                ws[32 * q : 32 * q + 4, :, :].bitcast(I32),
+                w_scales[:, :, 4 * q : 4 * q + 4, :].rearrange("e s b n -> b (e s) n").bitcast(I32),
+            )
+        nc.sync.dma_start(ww[:].bitcast(I32), w_words.rearrange("e s p n -> p (e s) n").bitcast(I32))
+        nc.sync.dma_start(wb_raw[:].rearrange("p f j n -> p f (j n)"), wb.rearrange("f (p j) n -> p f (j n)", j=PACK))
+        nc.sync.dma_start(q_sb[:], gate2)
+        nc.sync.dma_start(pos_sb[0][:], pos1)
+        nc.sync.dma_start(pos_sb[1][:], pos2)
+        nc.sync.dma_start(g_sb[0][:], gate[0])
+        load_wa(2, 1)
+        nc.sync.dma_start(g_sb[1][:], gate[1])
+        load_wa(3, 0)
+        load_wa(3, 1)
+
+        for a, b in ((0, 768), (768, 1536), (1536, 2048)):
+            nc.vector.tensor_copy(es[0][:, a:b], xs[:].indirect(offs_sb[:, a // PER_COL : b // PER_COL]))
+        for q in range(4):
+            nc.sync.dma_start(es[1][32 * q : 32 * q + 4, :].bitcast(I32), es[0][32 * q + 4 : 32 * q + 8, :].bitcast(I32))
+        as_sb = sb("as_sb", [P, F * D], U8)
+        nc.vector.tensor_copy(as_sb[:], xs[:].indirect(offs2_sb[:]))
+        aw = [sb("aw%d" % s, [P, F * D], U32) for s in range(PASSES)]
+        for s in range(PASSES):
+            nc.vector.tensor_copy(aw[s][:], xw[s][:].bitcast(U32).indirect(offs2_sb[:]))
+
+        wa_q = [[sb("wa_q%d%d" % (f, s), [P, H], U32) for s in range(PASSES)] for f in range(F)]
+        wa_s = [[sb("wa_s%d%d" % (f, s), [P, H], U8) for s in range(PASSES)] for f in range(F)]
+        wb_bf = sb("wb_bf", [P, F, N, PACK], BF16)
+        wb_q = sb("wb_q", [P, F * N], U32)
+        wb_s = sb("wb_s", [P, F * N], U8)
+        y_sb = sb("y_sb", [P, SLOTS], F32)
+        y_ps = [psum.tile([P, BANK], F32, name="y_ps%d" % c) for c in range(CHUNKS)]
+        h_ps = [psum.tile([P, PACK, D], F32, name="h_ps%d" % u) for u in range(2)]
+        z_ps = [psum.tile([P, D], F32, name="z_ps%d" % u) for u in range(2)]
+
+        def prep_wa(f, s):
+            wa_bf = sb("wa_bf%d%d" % (f, s), [P, PACK, P, PACK], BF16, tag="stage%d" % (f * PASSES + s))
+            width = P // pieces[f, s]
+            for u, raw in enumerate(wa_raw[f, s]):
+                nc.scalar.copy(
+                    wa_bf[:, :, u * width : (u + 1) * width, :].rearrange("p t m j -> p m j t"),
+                    raw[:].rearrange("p j (m t) -> p m j t", t=PACK),
+                )
+            nc.vector.quantize_mx(
+                out=wa_q[f][s][:].bitcast(FP8X4), scales=wa_s[f][s][:], in_=wa_bf[:].rearrange("p t m j -> p (t m j)")
+            )
+
+        def prep_wb():
+            nc.scalar.copy(
+                wb_bf[:].rearrange("p f (c i) j -> p f c j i", i=PACK),
+                wb_raw[:].rearrange("p f j (c i) -> p f c j i", i=PACK),
+            )
+            nc.vector.quantize_mx(out=wb_q[:].bitcast(FP8X4), scales=wb_s[:], in_=wb_bf[:].rearrange("p f n j -> p (f n j)"))
+
+        def experts(c):
+            ew = sb("ew%d" % c, [P, PASSES, BANK], U32, tag="stage%d" % (c + 1))
+            for s in range(PASSES):
+                picks = offs_sb[:, c * BANK // PER_COL : (c + 1) * BANK // PER_COL]
+                nc.vector.tensor_copy(ew[:, s, :], xw[s][:].bitcast(U32).indirect(picks))
+            for u in range(BANK // C):
+                e = c * (BANK // C) + u
+                cols = slice(u * C, (u + 1) * C)
+                for s in range(PASSES):
+                    nc.tensor.matmul_mx(
+                        out=y_ps[c][:, cols],
+                        lhsT=ww[:, e * PASSES + s, :].bitcast(FP4X4),
+                        lhsT_scale=ws[:, e * PASSES + s, :],
+                        rhs=ew[:, s, cols].bitcast(FP8X4),
+                        rhs_scale=es[s][:, e * C : (e + 1) * C],
+                        start=(s == 0),
+                        stop=(s == PASSES - 1),
+                    )
+
+        def y_out(c):
+            nc.scalar.copy(y_sb[:, c * BANK : (c + 1) * BANK], y_ps[c][:])
+
+        h_q = [sb("h_q%d" % f, [P, D], U32) for f in range(F)]
+        h_s = [sb("h_s%d" % f, [P, D], U8) for f in range(F)]
+
+        def adapter_up(f):
+            slots = slice(f * D, (f + 1) * D)
+            bank = h_ps[f % 2]
+            for t in range(PACK):
+                cols = slice(t * P, (t + 1) * P)
+                for s in range(PASSES):
+                    nc.tensor.matmul_mx(
+                        out=bank[:, t, :],
+                        lhsT=wa_q[f][s][:, cols].bitcast(FP8X4),
+                        lhsT_scale=wa_s[f][s][:, cols],
+                        rhs=aw[s][:, slots].bitcast(FP8X4),
+                        rhs_scale=as_sb[4 * s : P, slots],
+                        start=(s == 0),
+                        stop=(s == PASSES - 1),
+                    )
+            h_bf = sb("h_bf%d" % f, [P, D, PACK], BF16)
+            nc.scalar.activation(h_bf[:], bank[:].rearrange("p t m -> p m t"), SILU)
+            nc.vector.quantize_mx(out=h_q[f][:].bitcast(FP8X4), scales=h_s[f][:], in_=h_bf[:].rearrange("p m t -> p (m t)"))
+
+        def adapter_down(f):
+            slots = slice(f * D, (f + 1) * D)
+            nc.tensor.matmul_mx(
+                out=z_ps[f % 2][:],
+                lhsT=wb_q[:, f * N : (f + 1) * N].bitcast(FP8X4),
+                lhsT_scale=wb_s[:, f * N : (f + 1) * N],
+                rhs=h_q[f][:].bitcast(FP8X4),
+                rhs_scale=h_s[f][:],
+                start=True,
+                stop=True,
+            )
+            z_sb = sb("z_sb%d" % f, [P, D], F32)
+            nc.scalar.copy(z_sb[:], z_ps[f % 2][:])
+            nc.vector.tensor_tensor(
+                scattered[:].indirect(offs2_sb[:, f * D // PER_COL : (f + 1) * D // PER_COL]), z_sb[:], q_sb[:, slots], MULT
+            )
+
+        HALF = T // 2
+        o_sb = [sb("o_sb%d" % h, [P, HALF], F32) for h in range(2)]
+
+        parts = {}
+
+        def fetch(h, r, tag=""):
+            parts[h, r] = sb("part%d%d" % (h, r), [P, HALF], F32, tag=tag)
+            nc.vector.tensor_tensor(
+                parts[h, r][:],
+                y_sb[:].indirect(pos_sb[r][:, h * HALF // PER_COL : (h + 1) * HALF // PER_COL]),
+                g_sb[r][:, h * HALF : (h + 1) * HALF],
+                MULT,
+            )
+
+        def combine(h):
+            nc.vector.tensor_tensor(o_sb[h][:], parts[h, 0][:], parts[h, 1][:], ADD)
+
+        prep_wa(0, 0)
+        prep_wa(0, 1)
+        experts(0)
+        prep_wa(1, 0)
+        adapter_up(0)
+        experts(1)
+        prep_wa(1, 1)
+        experts(2)
+        prep_wa(2, 0)
+        adapter_up(1)
+        experts(3)
+        y_out(0)
+        y_out(1)
+        prep_wb()
+        y_out(2)
+        y_out(3)
+        adapter_down(0)
+        adapter_down(1)
+        fetch(0, 0)
+        fetch(1, 0)
+        prep_wa(2, 1)
+        fetch(0, 1, "stage5")
+        prep_wa(3, 0)
+        adapter_up(2)
+        combine(0)
+        prep_wa(3, 1)
+        adapter_down(2)
+        adapter_up(3)
+        adapter_down(3)
+        fetch(1, 1, "stage7")
+        combine(1)
+        for h in range(2):
+            toks = slice(h * HALF, (h + 1) * HALF)
+            res = sb("res%d" % h, [P, HALF], F32)
+            nc.vector.tensor_tensor(res[:], o_sb[h][:], scattered[:, toks], ADD)
+            nc.sync.dma_start(out[:, toks], res[:])

@@ -43,22 +43,22 @@ def tile_moe_mlr_silu_kernel(
         pos_sb = [sb("pos%d_sb" % r, [P, T // PER_COL], U16) for r in range(2)]
         xs = sb("xs", [P, T], U8)
         xw = [sb("xw%d" % s, [P, T], I32) for s in range(PASSES)]
-        ww = sb("ww", [P, E * PASSES, 2 * N], U8)
+        ww = [sb("ww%d" % u, [P, E, 2 * N], U8) for u in range(2)]
         ws = sb("ws", [P, E * PASSES, N], U8)
         es = [sb("es%d" % s, [P, SLOTS], U8) for s in range(PASSES)]
         scattered = sb("scattered", [P, T], F32)
         pieces = {(f, s): (2 if (f, s) in ((0, 0), (F - 1, PASSES - 1)) else 1) for f in range(F) for s in range(PASSES)}
         wa_raw = {
-            (f, s): [sb("wa_raw%d%d%d" % (f, s, u), [P, PACK, H // n], F32) for u in range(n)] for (f, s), n in pieces.items()
+            (f, s): [sb("wa_raw%d%d%d" % (f, s, u), [P, PACK, H // n], F32, tag="wa_raw%d%d%d" % (f, s, u)) for u in range(n)] for (f, s), n in pieces.items()
         }
         wb_raw = sb("wb_raw", [P, F, PACK, N], F32)
         g_sb = [sb("g%d" % r, [P, T], F32) for r in range(2)]
         q_sb = sb("q_sb", [P, F * D], F32)
 
-        nc.vector.memset(xs[:].bitcast(I32), 0)
+        nc.gpsimd.memset(xs[:].bitcast(I32), 0)
         nc.vector.memset(ws[:].rearrange("p a n -> p (a n)").bitcast(I32), 0)
         nc.vector.memset(es[1][:].bitcast(I32), 0)
-        nc.vector.memset(scattered[:], 0.0)
+        nc.gpsimd.memset(scattered[:], 0.0)
 
         def load_wa(f, s):
             width = H // pieces[f, s]
@@ -69,46 +69,48 @@ def tile_moe_mlr_silu_kernel(
         def load_xw(s):
             nc.sync.dma_start(xw[s][:], x_words[s].rearrange("p t d -> p (t d)").bitcast(I32))
 
+        as_sb = sb("as_sb", [P, F * D], U8)
+        aw = [sb("aw%d" % s, [P, F * D], U32) for s in range(PASSES)]
+
         nc.sync.dma_start(offs_sb[:], offs)
-        nc.sync.dma_start(offs2_sb[:], offs2)
         for q in range(4):
             nc.sync.dma_start(xs[32 * q : 32 * q + 8, :].bitcast(I32), x_scales[:, 4 * q : 4 * q + 4, :].bitcast(I32))
+        nc.sync.dma_start(offs2_sb[:], offs2)
         load_wa(0, 0)
-        load_xw(0)
         load_wa(0, 1)
+        load_xw(0)
         load_xw(1)
         load_wa(1, 0)
         load_wa(1, 1)
+        for a, b in ((0, 768), (768, 1536), (1536, 2048)):
+            nc.vector.tensor_copy(es[0][:, a:b], xs[:].indirect(offs_sb[:, a // PER_COL : b // PER_COL]))
+        nc.vector.tensor_copy(as_sb[:], xs[:].indirect(offs2_sb[:]))
+        for s in range(PASSES):
+            nc.vector.tensor_copy(aw[s][:], xw[s][:].bitcast(U32).indirect(offs2_sb[:]))
         load_wa(2, 0)
+        nc.sync.dma_start(pos_sb[0][:], pos1)
         for q in range(4):
-            nc.sync.dma_start(
+            nc.sync.dma_start(es[1][32 * q : 32 * q + 4, :].bitcast(I32), es[0][32 * q + 4 : 32 * q + 8, :].bitcast(I32))
+        for q in range(4):
+            nc.gpsimd.dma_start(
                 ws[32 * q : 32 * q + 4, :, :].bitcast(I32),
                 w_scales[:, :, 4 * q : 4 * q + 4, :].rearrange("e s b n -> b (e s) n").bitcast(I32),
             )
-        nc.sync.dma_start(ww[:].bitcast(I32), w_words.rearrange("e s p n -> p (e s) n").bitcast(I32))
         nc.sync.dma_start(wb_raw[:].rearrange("p f j n -> p f (j n)"), wb.rearrange("f (p j) n -> p f (j n)", j=PACK))
+        for u in range(2):
+            half = w_words[u * E // 2 : (u + 1) * E // 2]
+            nc.sync.dma_start(ww[u][:].bitcast(I32), half.rearrange("e s p n -> p (e s) n").bitcast(I32))
         nc.sync.dma_start(q_sb[:], gate2)
-        nc.sync.dma_start(pos_sb[0][:], pos1)
+        load_wa(2, 1)
         nc.sync.dma_start(pos_sb[1][:], pos2)
         nc.sync.dma_start(g_sb[0][:], gate[0])
-        load_wa(2, 1)
-        nc.sync.dma_start(g_sb[1][:], gate[1])
         load_wa(3, 0)
         load_wa(3, 1)
-
-        for a, b in ((0, 768), (768, 1536), (1536, 2048)):
-            nc.vector.tensor_copy(es[0][:, a:b], xs[:].indirect(offs_sb[:, a // PER_COL : b // PER_COL]))
-        for q in range(4):
-            nc.sync.dma_start(es[1][32 * q : 32 * q + 4, :].bitcast(I32), es[0][32 * q + 4 : 32 * q + 8, :].bitcast(I32))
-        as_sb = sb("as_sb", [P, F * D], U8)
-        nc.vector.tensor_copy(as_sb[:], xs[:].indirect(offs2_sb[:]))
-        aw = [sb("aw%d" % s, [P, F * D], U32) for s in range(PASSES)]
-        for s in range(PASSES):
-            nc.vector.tensor_copy(aw[s][:], xw[s][:].bitcast(U32).indirect(offs2_sb[:]))
+        nc.sync.dma_start(g_sb[1][:], gate[1])
 
         wa_q = [[sb("wa_q%d%d" % (f, s), [P, H], U32) for s in range(PASSES)] for f in range(F)]
         wa_s = [[sb("wa_s%d%d" % (f, s), [P, H], U8) for s in range(PASSES)] for f in range(F)]
-        wb_bf = sb("wb_bf", [P, F, N, PACK], BF16)
+        wb_bf = sb("wb_bf", [P, F, N, PACK], BF16, tag="wb_bf")
         wb_q = sb("wb_q", [P, F * N], U32)
         wb_s = sb("wb_s", [P, F * N], U8)
         y_sb = sb("y_sb", [P, SLOTS], F32)
@@ -136,7 +138,7 @@ def tile_moe_mlr_silu_kernel(
             nc.vector.quantize_mx(out=wb_q[:].bitcast(FP8X4), scales=wb_s[:], in_=wb_bf[:].rearrange("p f n j -> p (f n j)"))
 
         def experts(c):
-            ew = sb("ew%d" % c, [P, PASSES, BANK], U32, tag="stage%d" % (c + 1))
+            ew = sb("ew%d" % c, [P, PASSES, BANK], U32, tag="stage%d" % (c + 1) if c < CHUNKS - 1 else "wb_bf")
             for s in range(PASSES):
                 picks = offs_sb[:, c * BANK // PER_COL : (c + 1) * BANK // PER_COL]
                 nc.vector.tensor_copy(ew[:, s, :], xw[s][:].bitcast(U32).indirect(picks))
@@ -146,7 +148,7 @@ def tile_moe_mlr_silu_kernel(
                 for s in range(PASSES):
                     nc.tensor.matmul_mx(
                         out=y_ps[c][:, cols],
-                        lhsT=ww[:, e * PASSES + s, :].bitcast(FP4X4),
+                        lhsT=ww[2 * e // E][:, (e * PASSES + s) % E, :].bitcast(FP4X4),
                         lhsT_scale=ws[:, e * PASSES + s, :],
                         rhs=ew[:, s, cols].bitcast(FP8X4),
                         rhs_scale=es[s][:, e * C : (e + 1) * C],
@@ -155,7 +157,10 @@ def tile_moe_mlr_silu_kernel(
                     )
 
         def y_out(c):
-            nc.scalar.copy(y_sb[:, c * BANK : (c + 1) * BANK], y_ps[c][:])
+            if c == CHUNKS - 1:
+                nc.vector.tensor_copy(y_sb[:, c * BANK : (c + 1) * BANK], y_ps[c][:])
+            else:
+                nc.scalar.copy(y_sb[:, c * BANK : (c + 1) * BANK], y_ps[c][:])
 
         h_q = [sb("h_q%d" % f, [P, D], U32) for f in range(F)]
         h_s = [sb("h_s%d" % f, [P, D], U8) for f in range(F)]
@@ -175,7 +180,7 @@ def tile_moe_mlr_silu_kernel(
                         start=(s == 0),
                         stop=(s == PASSES - 1),
                     )
-            h_bf = sb("h_bf%d" % f, [P, D, PACK], BF16)
+            h_bf = sb("h_bf%d" % f, [P, D, PACK], BF16, tag="wa_raw%d00" % (f + 1) if f < F - 1 else "h_bf3")
             nc.scalar.activation(h_bf[:], bank[:].rearrange("p t m -> p m t"), SILU)
             nc.vector.quantize_mx(out=h_q[f][:].bitcast(FP8X4), scales=h_s[f][:], in_=h_bf[:].rearrange("p m t -> p (m t)"))
 
@@ -190,14 +195,14 @@ def tile_moe_mlr_silu_kernel(
                 start=True,
                 stop=True,
             )
-            z_sb = sb("z_sb%d" % f, [P, D], F32)
+            z_sb = sb("z_sb%d" % f, [P, D], F32, tag="wa_raw311" if f == 2 else "")
             nc.scalar.copy(z_sb[:], z_ps[f % 2][:])
             nc.vector.tensor_tensor(
                 scattered[:].indirect(offs2_sb[:, f * D // PER_COL : (f + 1) * D // PER_COL]), z_sb[:], q_sb[:, slots], MULT
             )
 
         HALF = T // 2
-        o_sb = [sb("o_sb%d" % h, [P, HALF], F32) for h in range(2)]
+        o_sb = {}
 
         parts = {}
 
@@ -210,7 +215,8 @@ def tile_moe_mlr_silu_kernel(
                 MULT,
             )
 
-        def combine(h):
+        def combine(h, tag=""):
+            o_sb[h] = sb("o_sb%d" % h, [P, HALF], F32, tag=tag)
             nc.vector.tensor_tensor(o_sb[h][:], parts[h, 0][:], parts[h, 1][:], ADD)
 
         prep_wa(0, 0)
@@ -222,28 +228,28 @@ def tile_moe_mlr_silu_kernel(
         prep_wa(1, 1)
         experts(2)
         prep_wa(2, 0)
+        prep_wb()
         adapter_up(1)
         experts(3)
-        y_out(0)
-        y_out(1)
-        prep_wb()
-        y_out(2)
-        y_out(3)
         adapter_down(0)
         adapter_down(1)
-        fetch(0, 0)
-        fetch(1, 0)
+        y_out(0)
+        y_out(1)
+        y_out(2)
+        y_out(3)
         prep_wa(2, 1)
-        fetch(0, 1, "stage5")
+        fetch(0, 0)
+        fetch(1, 0, "stage5")
         prep_wa(3, 0)
         adapter_up(2)
-        combine(0)
         prep_wa(3, 1)
         adapter_down(2)
         adapter_up(3)
         adapter_down(3)
+        fetch(0, 1, "stage6")
+        combine(0)
         fetch(1, 1, "stage7")
-        combine(1)
+        combine(1, "h_bf3")
         for h in range(2):
             toks = slice(h * HALF, (h + 1) * HALF)
             res = sb("res%d" % h, [P, HALF], F32)

@@ -1,6 +1,7 @@
 from contextlib import ExitStack
 
 import concourse.mybir as mybir
+from concourse.masks import make_identity
 
 K, T, E, C, F, D, H, N = 1024, 1024, 16, 128, 4, 128, 512, 128
 FLOPS = 2 * K * N * E * C + 2 * K * H * F * D + 2 * H * N * F * D
@@ -25,6 +26,8 @@ SLOTS = E * C
 BANK = 512
 CHUNKS = SLOTS // BANK
 PER_COL = 16
+HALVED = ((0, 0), (3, 0), (3, 1))
+ON_VECTOR = {(3, 0, 1): 256, (3, 1, 0): 256, (3, 1, 1): 128}
 
 
 def tile_moe_mlr_silu_kernel(
@@ -47,24 +50,31 @@ def tile_moe_mlr_silu_kernel(
         ws = sb("ws", [P, E * PASSES, N], U8)
         es = [sb("es%d" % s, [P, SLOTS], U8) for s in range(PASSES)]
         scattered = sb("scattered", [P, T], F32)
-        pieces = {(f, s): (2 if (f, s) in ((0, 0), (F - 1, PASSES - 1)) else 1) for f in range(F) for s in range(PASSES)}
+        pieces = {(f, s): (2 if (f, s) in HALVED else 1) for f in range(F) for s in range(PASSES)}
         wa_raw = {
             (f, s): [sb("wa_raw%d%d%d" % (f, s, u), [P, PACK, H // n], F32, tag="wa_raw%d%d%d" % (f, s, u)) for u in range(n)] for (f, s), n in pieces.items()
         }
-        wb_raw = sb("wb_raw", [P, F, PACK, N], F32)
-        g_sb = [sb("g%d" % r, [P, T], F32) for r in range(2)]
+        wb_raw = sb("wb_raw", [P, F, PACK, N], F32, tag="wb_raw")
+        g_sb = [[sb("g%d%d" % (h, r), [P, T // 2], F32) for r in range(2)] for h in range(2)]
+        ident = sb("ident", [P, P], F32)
         q_sb = sb("q_sb", [P, F * D], F32)
 
         nc.gpsimd.memset(xs[:].bitcast(I32), 0)
         nc.vector.memset(ws[:].rearrange("p a n -> p (a n)").bitcast(I32), 0)
         nc.vector.memset(es[1][:].bitcast(I32), 0)
+        make_identity(nc, ident[:])
         nc.gpsimd.memset(scattered[:], 0.0)
 
-        def load_wa(f, s):
+        def load_wa(f, s, only=None):
             width = H // pieces[f, s]
             for u, raw in enumerate(wa_raw[f, s]):
+                if only is not None and u != only:
+                    continue
                 src = wa[f, s * PASS : (s + 1) * PASS, u * width : (u + 1) * width]
                 nc.sync.dma_start(raw[:], src.rearrange("(p j) c -> p j c", j=PACK))
+
+        def load_gate(h, r):
+            nc.sync.dma_start(g_sb[h][r][:], gate[r, :, h * T // 2 : (h + 1) * T // 2])
 
         def load_xw(s):
             nc.sync.dma_start(xw[s][:], x_words[s].rearrange("p t d -> p (t d)").bitcast(I32))
@@ -87,8 +97,9 @@ def tile_moe_mlr_silu_kernel(
         nc.vector.tensor_copy(as_sb[:], xs[:].indirect(offs2_sb[:]))
         for s in range(PASSES):
             nc.vector.tensor_copy(aw[s][:], xw[s][:].bitcast(U32).indirect(offs2_sb[:]))
-        load_wa(2, 0)
+        nc.sync.dma_start(wb_raw[:].rearrange("p f j n -> p f (j n)"), wb.rearrange("f (p j) n -> p f (j n)", j=PACK))
         nc.sync.dma_start(pos_sb[0][:], pos1)
+        nc.sync.dma_start(pos_sb[1][:], pos2)
         for q in range(4):
             nc.sync.dma_start(es[1][32 * q : 32 * q + 4, :].bitcast(I32), es[0][32 * q + 4 : 32 * q + 8, :].bitcast(I32))
         for q in range(4):
@@ -96,17 +107,18 @@ def tile_moe_mlr_silu_kernel(
                 ws[32 * q : 32 * q + 4, :, :].bitcast(I32),
                 w_scales[:, :, 4 * q : 4 * q + 4, :].rearrange("e s b n -> b (e s) n").bitcast(I32),
             )
-        nc.sync.dma_start(wb_raw[:].rearrange("p f j n -> p f (j n)"), wb.rearrange("f (p j) n -> p f (j n)", j=PACK))
         for u in range(2):
             half = w_words[u * E // 2 : (u + 1) * E // 2]
             nc.sync.dma_start(ww[u][:].bitcast(I32), half.rearrange("e s p n -> p (e s) n").bitcast(I32))
         nc.sync.dma_start(q_sb[:], gate2)
+        load_gate(0, 0)
+        load_wa(2, 0)
+        load_gate(0, 1)
         load_wa(2, 1)
-        nc.sync.dma_start(pos_sb[1][:], pos2)
-        nc.sync.dma_start(g_sb[0][:], gate[0])
+        load_gate(1, 0)
         load_wa(3, 0)
         load_wa(3, 1)
-        nc.sync.dma_start(g_sb[1][:], gate[1])
+        load_gate(1, 1)
 
         wa_q = [[sb("wa_q%d%d" % (f, s), [P, H], U32) for s in range(PASSES)] for f in range(F)]
         wa_s = [[sb("wa_s%d%d" % (f, s), [P, H], U8) for s in range(PASSES)] for f in range(F)]
@@ -114,21 +126,29 @@ def tile_moe_mlr_silu_kernel(
         wb_q = sb("wb_q", [P, F * N], U32)
         wb_s = sb("wb_s", [P, F * N], U8)
         y_sb = sb("y_sb", [P, SLOTS], F32)
-        y_ps = [psum.tile([P, BANK], F32, name="y_ps%d" % c) for c in range(CHUNKS)]
-        h_ps = [psum.tile([P, PACK, D], F32, name="h_ps%d" % u) for u in range(2)]
-        z_ps = [psum.tile([P, D], F32, name="z_ps%d" % u) for u in range(2)]
+        y_ps = [psum.tile([P, BANK], F32, name="y_ps%d" % c, tag="bank%d" % c) for c in range(CHUNKS)]
+        h_ps = [psum.tile([P, H], F32, name="h_ps%d" % u) for u in range(2)]
+        turn_ps = psum.tile([P, 2, D], F32, name="turn_ps")
 
         def prep_wa(f, s):
-            wa_bf = sb("wa_bf%d%d" % (f, s), [P, PACK, P, PACK], BF16, tag="stage%d" % (f * PASSES + s))
-            width = P // pieces[f, s]
+            wa_bf = sb("wa_bf%d%d" % (f, s), [P, H, PACK], BF16, tag="stage%d" % (f * PASSES + s))
+            width = H // pieces[f, s]
             for u, raw in enumerate(wa_raw[f, s]):
-                nc.scalar.copy(
-                    wa_bf[:, :, u * width : (u + 1) * width, :].rearrange("p t m j -> p m j t"),
-                    raw[:].rearrange("p j (m t) -> p m j t", t=PACK),
+                share = ON_VECTOR.get((f, s, u), 0)
+                for cast, a, b in ((nc.scalar.copy, 0, width - share), (nc.vector.tensor_copy, width - share, width)):
+                    if b > a:
+                        cast(
+                            wa_bf[:, u * width + a : u * width + b, :].rearrange("p (c i) j -> p c j i", i=PACK),
+                            raw[:, :, a:b].rearrange("p j (c i) -> p c j i", i=PACK),
+                        )
+            width = H // (pieces[f, s] if (f, s) == (F - 1, PASSES - 1) else 1)
+            for c0 in range(0, H, width):
+                cols = slice(c0, c0 + width)
+                nc.vector.quantize_mx(
+                    out=wa_q[f][s][:, cols].bitcast(FP8X4),
+                    scales=wa_s[f][s][:, cols],
+                    in_=wa_bf[:, cols, :].rearrange("p c j -> p (c j)"),
                 )
-            nc.vector.quantize_mx(
-                out=wa_q[f][s][:].bitcast(FP8X4), scales=wa_s[f][s][:], in_=wa_bf[:].rearrange("p t m j -> p (t m j)")
-            )
 
         def prep_wb():
             nc.scalar.copy(
@@ -137,8 +157,8 @@ def tile_moe_mlr_silu_kernel(
             )
             nc.vector.quantize_mx(out=wb_q[:].bitcast(FP8X4), scales=wb_s[:], in_=wb_bf[:].rearrange("p f n j -> p (f n j)"))
 
-        def experts(c):
-            ew = sb("ew%d" % c, [P, PASSES, BANK], U32, tag="stage%d" % (c + 1) if c < CHUNKS - 1 else "wb_bf")
+        def experts(c, tag):
+            ew = sb("ew%d" % c, [P, PASSES, BANK], U32, tag=tag)
             for s in range(PASSES):
                 picks = offs_sb[:, c * BANK // PER_COL : (c + 1) * BANK // PER_COL]
                 nc.vector.tensor_copy(ew[:, s, :], xw[s][:].bitcast(U32).indirect(picks))
@@ -165,29 +185,40 @@ def tile_moe_mlr_silu_kernel(
         h_q = [sb("h_q%d" % f, [P, D], U32) for f in range(F)]
         h_s = [sb("h_s%d" % f, [P, D], U8) for f in range(F)]
 
-        def adapter_up(f):
+        def adapter_up(f, silu_tag="", turn_tag=None):
             slots = slice(f * D, (f + 1) * D)
-            bank = h_ps[f % 2]
-            for t in range(PACK):
-                cols = slice(t * P, (t + 1) * P)
-                for s in range(PASSES):
+            turns = range(PASSES) if f == F - 1 else range(PASSES - 1, -1, -1)
+            h_rows = sb("h_rows%d" % f, [P, H], BF16, tag=silu_tag)
+            width = H // (pieces[f, PASSES - 1] if f == F - 1 else 1)
+            for c0 in range(0, H, width):
+                cols = slice(c0, c0 + width)
+                bank = h_ps[(f + c0 // width) % 2]
+                for s in turns:
                     nc.tensor.matmul_mx(
-                        out=bank[:, t, :],
-                        lhsT=wa_q[f][s][:, cols].bitcast(FP8X4),
-                        lhsT_scale=wa_s[f][s][:, cols],
-                        rhs=aw[s][:, slots].bitcast(FP8X4),
-                        rhs_scale=as_sb[4 * s : P, slots],
-                        start=(s == 0),
-                        stop=(s == PASSES - 1),
+                        out=bank[:, cols],
+                        lhsT=aw[s][:, slots].bitcast(FP8X4),
+                        lhsT_scale=as_sb[4 * s : P, slots],
+                        rhs=wa_q[f][s][:, cols].bitcast(FP8X4),
+                        rhs_scale=wa_s[f][s][:, cols],
+                        start=(s == turns[0]),
+                        stop=(s == turns[-1]),
                     )
-            h_bf = sb("h_bf%d" % f, [P, D, PACK], BF16, tag="wa_raw%d00" % (f + 1) if f < F - 1 else "h_bf3")
-            nc.scalar.activation(h_bf[:], bank[:].rearrange("p t m -> p m t"), SILU)
+                nc.scalar.activation(h_rows[:, cols], bank[:, cols], SILU)
+            pairs = h_rows[:].bitcast(F32)
+            for u in range(2):
+                nc.tensor.transpose(turn_ps[:, u, :], pairs[:, u : H // 2 : 2], ident[:])
+            h_bf = sb("h_bf%d" % f, [P, D, PACK], BF16, tag=turn_tag or "h_bf%d" % f)
+            nc.scalar.copy(
+                h_bf[:].rearrange("p m t -> p (m t)").bitcast(F32).rearrange("p (m u) -> p m u", u=2),
+                turn_ps[:].rearrange("p u m -> p m u"),
+            )
             nc.vector.quantize_mx(out=h_q[f][:].bitcast(FP8X4), scales=h_s[f][:], in_=h_bf[:].rearrange("p m t -> p (m t)"))
 
-        def adapter_down(f):
+        def adapter_down(f, tag=""):
             slots = slice(f * D, (f + 1) * D)
+            z_ps = psum.tile([P, D], F32, name="z_ps%d" % f, tag="bank%d" % (2 * f % CHUNKS))
             nc.tensor.matmul_mx(
-                out=z_ps[f % 2][:],
+                out=z_ps[:],
                 lhsT=wb_q[:, f * N : (f + 1) * N].bitcast(FP8X4),
                 lhsT_scale=wb_s[:, f * N : (f + 1) * N],
                 rhs=h_q[f][:].bitcast(FP8X4),
@@ -195,8 +226,8 @@ def tile_moe_mlr_silu_kernel(
                 start=True,
                 stop=True,
             )
-            z_sb = sb("z_sb%d" % f, [P, D], F32, tag="wa_raw311" if f == 2 else "")
-            nc.scalar.copy(z_sb[:], z_ps[f % 2][:])
+            z_sb = sb("z_sb%d" % f, [P, D], F32, tag=tag)
+            nc.scalar.copy(z_sb[:], z_ps[:])
             nc.vector.tensor_tensor(
                 scattered[:].indirect(offs2_sb[:, f * D // PER_COL : (f + 1) * D // PER_COL]), z_sb[:], q_sb[:, slots], MULT
             )
@@ -211,7 +242,7 @@ def tile_moe_mlr_silu_kernel(
             nc.vector.tensor_tensor(
                 parts[h, r][:],
                 y_sb[:].indirect(pos_sb[r][:, h * HALF // PER_COL : (h + 1) * HALF // PER_COL]),
-                g_sb[r][:, h * HALF : (h + 1) * HALF],
+                g_sb[h][r][:],
                 MULT,
             )
 
@@ -221,33 +252,33 @@ def tile_moe_mlr_silu_kernel(
 
         prep_wa(0, 0)
         prep_wa(0, 1)
-        experts(0)
+        experts(0, "stage1")
         prep_wa(1, 0)
-        adapter_up(0)
-        experts(1)
+        experts(1, "stage2")
         prep_wa(1, 1)
-        experts(2)
-        prep_wa(2, 0)
+        adapter_up(0, "wa_raw110")
+        experts(2, "stage3")
         prep_wb()
-        adapter_up(1)
-        experts(3)
-        adapter_down(0)
-        adapter_down(1)
         y_out(0)
+        adapter_up(1, "wb_raw")
+        adapter_down(0)
         y_out(1)
+        experts(3, "h_bf0")
         y_out(2)
+        adapter_down(1)
         y_out(3)
-        prep_wa(2, 1)
         fetch(0, 0)
-        fetch(1, 0, "stage5")
+        fetch(0, 1)
+        prep_wa(2, 0)
+        combine(0, "stage4")
+        prep_wa(2, 1)
+        fetch(1, 0)
         prep_wa(3, 0)
-        adapter_up(2)
         prep_wa(3, 1)
-        adapter_down(2)
+        adapter_up(2, "wa_raw300", "wa_raw311")
         adapter_up(3)
+        adapter_down(2)
         adapter_down(3)
-        fetch(0, 1, "stage6")
-        combine(0)
         fetch(1, 1, "stage7")
         combine(1, "h_bf3")
         for h in range(2):

@@ -26,8 +26,9 @@ SLOTS = E * C
 BANK = 512
 CHUNKS = SLOTS // BANK
 PER_COL = 16
-HALVED = ((0, 0), (3, 0), (3, 1))
-ON_VECTOR = {(3, 0, 1): 256, (3, 1, 0): 256, (3, 1, 1): 128}
+LAST_SPLIT = 1
+HALVED = ()
+ON_VECTOR = {(2, 1, 0): 256, (3, 0, 0): 256, (3, 1, 0): 384}
 
 
 def tile_moe_mlr_silu_kernel(
@@ -54,14 +55,17 @@ def tile_moe_mlr_silu_kernel(
         wa_raw = {
             (f, s): [sb("wa_raw%d%d%d" % (f, s, u), [P, PACK, H // n], F32, tag="wa_raw%d%d%d" % (f, s, u)) for u in range(n)] for (f, s), n in pieces.items()
         }
-        wb_raw = sb("wb_raw", [P, F, PACK, N], F32, tag="wb_raw")
+        wb_raw = [sb("wb_raw%d" % u, [P, F // 2, PACK, N], F32, tag="wb_raw%d" % u) for u in range(2)]
         g_sb = [[sb("g%d%d" % (h, r), [P, T // 2], F32) for r in range(2)] for h in range(2)]
+        g_rows = sb("g_rows", [P, P], F32, tag="g_rows")
+        g_cols = sb("g_cols", [P, 2 * T // P], F32)
         ident = sb("ident", [P, P], F32)
         q_sb = sb("q_sb", [P, F * D], F32)
 
         nc.gpsimd.memset(xs[:].bitcast(I32), 0)
         nc.vector.memset(ws[:].rearrange("p a n -> p (a n)").bitcast(I32), 0)
         nc.vector.memset(es[1][:].bitcast(I32), 0)
+        nc.gpsimd.memset(g_rows[:], 0.0)
         make_identity(nc, ident[:])
         nc.gpsimd.memset(scattered[:], 0.0)
 
@@ -73,8 +77,9 @@ def tile_moe_mlr_silu_kernel(
                 src = wa[f, s * PASS : (s + 1) * PASS, u * width : (u + 1) * width]
                 nc.sync.dma_start(raw[:], src.rearrange("(p j) c -> p j c", j=PACK))
 
-        def load_gate(h, r):
-            nc.sync.dma_start(g_sb[h][r][:], gate[r, :, h * T // 2 : (h + 1) * T // 2])
+        def load_wb(u):
+            half = wb[u * F // 2 : (u + 1) * F // 2]
+            nc.sync.dma_start(wb_raw[u][:].rearrange("p f j n -> p f (j n)"), half.rearrange("f (p j) n -> p f (j n)", j=PACK))
 
         def load_xw(s):
             nc.sync.dma_start(xw[s][:], x_words[s].rearrange("p t d -> p (t d)").bitcast(I32))
@@ -88,45 +93,42 @@ def tile_moe_mlr_silu_kernel(
         nc.sync.dma_start(offs2_sb[:], offs2)
         load_wa(0, 0)
         load_wa(0, 1)
+        nc.sync.dma_start(g_rows[0 : 2 * T // P, :], gate[:, 0, :].rearrange("r (b p) -> r b p", p=P))
         load_xw(0)
         load_xw(1)
+        for r in range(4):
+            nc.sync.dma_start(
+                ws[r:P:32, :, :].bitcast(I32),
+                w_scales[:, :, r:16:4, :].rearrange("e s b n -> b (e s) n").bitcast(I32),
+            )
         load_wa(1, 0)
-        load_wa(1, 1)
         for a, b in ((0, 768), (768, 1536), (1536, 2048)):
             nc.vector.tensor_copy(es[0][:, a:b], xs[:].indirect(offs_sb[:, a // PER_COL : b // PER_COL]))
         nc.vector.tensor_copy(as_sb[:], xs[:].indirect(offs2_sb[:]))
         for s in range(PASSES):
             nc.vector.tensor_copy(aw[s][:], xw[s][:].bitcast(U32).indirect(offs2_sb[:]))
-        nc.sync.dma_start(wb_raw[:].rearrange("p f j n -> p f (j n)"), wb.rearrange("f (p j) n -> p f (j n)", j=PACK))
         nc.sync.dma_start(pos_sb[0][:], pos1)
         nc.sync.dma_start(pos_sb[1][:], pos2)
-        for q in range(4):
-            nc.sync.dma_start(es[1][32 * q : 32 * q + 4, :].bitcast(I32), es[0][32 * q + 4 : 32 * q + 8, :].bitcast(I32))
-        for q in range(4):
-            nc.gpsimd.dma_start(
-                ws[32 * q : 32 * q + 4, :, :].bitcast(I32),
-                w_scales[:, :, 4 * q : 4 * q + 4, :].rearrange("e s b n -> b (e s) n").bitcast(I32),
-            )
+        for r in range(4):
+            nc.sync.dma_start(es[1][r:P:32, :].bitcast(I32), es[0][4 + r : P : 32, :].bitcast(I32))
         for u in range(2):
             half = w_words[u * E // 2 : (u + 1) * E // 2]
             nc.sync.dma_start(ww[u][:].bitcast(I32), half.rearrange("e s p n -> p (e s) n").bitcast(I32))
-        nc.sync.dma_start(q_sb[:], gate2)
-        load_gate(0, 0)
+        load_wa(1, 1)
         load_wa(2, 0)
-        load_gate(0, 1)
         load_wa(2, 1)
-        load_gate(1, 0)
         load_wa(3, 0)
         load_wa(3, 1)
-        load_gate(1, 1)
+        load_wb(0)
+        nc.sync.dma_start(q_sb[:], gate2)
+        load_wb(1)
 
         wa_q = [[sb("wa_q%d%d" % (f, s), [P, H], U32) for s in range(PASSES)] for f in range(F)]
         wa_s = [[sb("wa_s%d%d" % (f, s), [P, H], U8) for s in range(PASSES)] for f in range(F)]
-        wb_bf = sb("wb_bf", [P, F, N, PACK], BF16, tag="wb_bf")
-        wb_q = sb("wb_q", [P, F * N], U32)
-        wb_s = sb("wb_s", [P, F * N], U8)
+        wb_q = [sb("wb_q%d" % u, [P, F * N // 2], U32) for u in range(2)]
+        wb_s = [sb("wb_s%d" % u, [P, F * N // 2], U8) for u in range(2)]
         y_sb = sb("y_sb", [P, SLOTS], F32)
-        y_ps = [psum.tile([P, BANK], F32, name="y_ps%d" % c, tag="bank%d" % c) for c in range(CHUNKS)]
+        y_ps = {}
         h_ps = [psum.tile([P, H], F32, name="h_ps%d" % u) for u in range(2)]
         turn_ps = psum.tile([P, 2, D], F32, name="turn_ps")
 
@@ -141,7 +143,7 @@ def tile_moe_mlr_silu_kernel(
                             wa_bf[:, u * width + a : u * width + b, :].rearrange("p (c i) j -> p c j i", i=PACK),
                             raw[:, :, a:b].rearrange("p j (c i) -> p c j i", i=PACK),
                         )
-            width = H // (pieces[f, s] if (f, s) == (F - 1, PASSES - 1) else 1)
+            width = H // (LAST_SPLIT if (f, s) == (F - 1, PASSES - 1) else 1)
             for c0 in range(0, H, width):
                 cols = slice(c0, c0 + width)
                 nc.vector.quantize_mx(
@@ -150,18 +152,31 @@ def tile_moe_mlr_silu_kernel(
                     in_=wa_bf[:, cols, :].rearrange("p c j -> p (c j)"),
                 )
 
-        def prep_wb():
-            nc.scalar.copy(
+        def prep_wb(u, cast):
+            wb_bf = sb("wb_bf%d" % u, [P, F // 2, N, PACK], BF16, tag="wb_bf%d" % u)
+            cast(
                 wb_bf[:].rearrange("p f (c i) j -> p f c j i", i=PACK),
-                wb_raw[:].rearrange("p f j (c i) -> p f c j i", i=PACK),
+                wb_raw[u][:].rearrange("p f j (c i) -> p f c j i", i=PACK),
             )
-            nc.vector.quantize_mx(out=wb_q[:].bitcast(FP8X4), scales=wb_s[:], in_=wb_bf[:].rearrange("p f n j -> p (f n j)"))
+            nc.vector.quantize_mx(out=wb_q[u][:].bitcast(FP8X4), scales=wb_s[u][:], in_=wb_bf[:].rearrange("p f n j -> p (f n j)"))
+
+        def gate_columns():
+            nc.tensor.transpose(turn_ps[:, 0, :], g_rows[:], ident[:])
+            nc.scalar.copy(g_cols[:], turn_ps[:, 0, 0 : 2 * T // P])
+
+        def spread_gate(h, r):
+            g_ps = psum.tile([P, T // 2], F32, name="g_ps%d%d" % (h, r), tag="bank%d" % (2 * h + r))
+            for b in range(T // 2 // P):
+                j = (r * T + h * T // 2) // P + b
+                nc.tensor.transpose(g_ps[:, b * P : (b + 1) * P], g_cols[:, j : j + 1].to_broadcast([P, P]), ident[:])
+            nc.scalar.copy(g_sb[h][r][:], g_ps[:])
 
         def experts(c, tag):
             ew = sb("ew%d" % c, [P, PASSES, BANK], U32, tag=tag)
             for s in range(PASSES):
                 picks = offs_sb[:, c * BANK // PER_COL : (c + 1) * BANK // PER_COL]
                 nc.vector.tensor_copy(ew[:, s, :], xw[s][:].bitcast(U32).indirect(picks))
+            y_ps[c] = psum.tile([P, BANK], F32, name="y_ps%d" % c, tag="bank%d" % c)
             for u in range(BANK // C):
                 e = c * (BANK // C) + u
                 cols = slice(u * C, (u + 1) * C)
@@ -189,7 +204,7 @@ def tile_moe_mlr_silu_kernel(
             slots = slice(f * D, (f + 1) * D)
             turns = range(PASSES) if f == F - 1 else range(PASSES - 1, -1, -1)
             h_rows = sb("h_rows%d" % f, [P, H], BF16, tag=silu_tag)
-            width = H // (pieces[f, PASSES - 1] if f == F - 1 else 1)
+            width = H // (LAST_SPLIT if f == F - 1 else 1)
             for c0 in range(0, H, width):
                 cols = slice(c0, c0 + width)
                 bank = h_ps[(f + c0 // width) % 2]
@@ -216,11 +231,11 @@ def tile_moe_mlr_silu_kernel(
 
         def adapter_down(f, tag=""):
             slots = slice(f * D, (f + 1) * D)
-            z_ps = psum.tile([P, D], F32, name="z_ps%d" % f, tag="bank%d" % (2 * f % CHUNKS))
+            z_ps = psum.tile([P, D], F32, name="z_ps%d" % f, tag="bank%d" % f)
             nc.tensor.matmul_mx(
                 out=z_ps[:],
-                lhsT=wb_q[:, f * N : (f + 1) * N].bitcast(FP8X4),
-                lhsT_scale=wb_s[:, f * N : (f + 1) * N],
+                lhsT=wb_q[f // 2][:, f % 2 * N : (f % 2 + 1) * N].bitcast(FP8X4),
+                lhsT_scale=wb_s[f // 2][:, f % 2 * N : (f % 2 + 1) * N],
                 rhs=h_q[f][:].bitcast(FP8X4),
                 rhs_scale=h_s[f][:],
                 start=True,
@@ -252,35 +267,40 @@ def tile_moe_mlr_silu_kernel(
 
         prep_wa(0, 0)
         prep_wa(0, 1)
+        gate_columns()
+        for h in range(2):
+            for r in range(2):
+                spread_gate(h, r)
         experts(0, "stage1")
+        experts(1, "wa_raw010")
         prep_wa(1, 0)
-        experts(1, "stage2")
-        prep_wa(1, 1)
-        adapter_up(0, "wa_raw110")
-        experts(2, "stage3")
-        prep_wb()
+        adapter_up(0, "wa_raw100")
+        experts(2, "stage2")
+        experts(3, "g_rows")
         y_out(0)
-        adapter_up(1, "wb_raw")
-        adapter_down(0)
         y_out(1)
-        experts(3, "h_bf0")
         y_out(2)
-        adapter_down(1)
         y_out(3)
         fetch(0, 0)
         fetch(0, 1)
+        prep_wa(1, 1)
+        combine(0, "stage3")
+        fetch(1, 0, "wa_raw110")
         prep_wa(2, 0)
-        combine(0, "stage4")
+        adapter_up(1, "wa_raw200")
         prep_wa(2, 1)
-        fetch(1, 0)
+        fetch(1, 1, "stage4")
         prep_wa(3, 0)
         prep_wa(3, 1)
-        adapter_up(2, "wa_raw300", "wa_raw311")
+        adapter_up(2, "wa_raw300", "wa_raw310")
         adapter_up(3)
+        combine(1, "stage7")
+        prep_wb(0, nc.scalar.copy)
+        prep_wb(1, nc.vector.tensor_copy)
+        adapter_down(0)
+        adapter_down(1)
         adapter_down(2)
         adapter_down(3)
-        fetch(1, 1, "stage7")
-        combine(1, "h_bf3")
         for h in range(2):
             toks = slice(h * HALF, (h + 1) * HALF)
             res = sb("res%d" % h, [P, HALF], F32)

from contextlib import ExitStack

import concourse.mybir as mybir
from concourse.masks import make_identity

K, T, E, C, F, D, H, N = 1024, 1024, 16, 128, 4, 128, 512, 128
FLOPS = 2 * K * N * E * C + 2 * K * H * F * D + 2 * H * N * F * D

F32 = mybir.dt.float32
BF16 = mybir.dt.bfloat16
I32 = mybir.dt.int32
U32 = mybir.dt.uint32
U16 = mybir.dt.uint16
U8 = mybir.dt.uint8
FP8X4 = mybir.dt.float8_e4m3fn_x4
FP4X4 = mybir.dt.float4_e2m1fn_x4
MULT = mybir.AluOpType.mult
ADD = mybir.AluOpType.add
SILU = mybir.ActivationFunctionType.Silu

P = 128
PACK = 4
PASS = P * PACK
PASSES = K // PASS
SLOTS = E * C
BANK = 512
CHUNKS = SLOTS // BANK
PER_COL = 16
LAST_SPLIT = 1
HALVED = ()
ON_VECTOR = {(2, 1, 0): 256, (3, 0, 0): 256, (3, 1, 0): 384}


def tile_moe_mlr_silu_kernel(
    tc, x_words, x_scales, w_words, w_scales, wa, wb, gate, gate2, offs, pos1, pos2, offs2, out
):
    nc = tc.nc
    with ExitStack() as ctx:
        keep = ctx.enter_context(tc.tile_pool(name="keep", bufs=1))
        psum = ctx.enter_context(tc.psum_pool(name="psum", bufs=1))

        def sb(name, shape, dtype, tag=""):
            return keep.tile(shape, dtype, name=name, align_bytes=64, tag=tag)

        offs_sb = sb("offs_sb", [P, SLOTS // PER_COL], U16)
        offs2_sb = sb("offs2_sb", [P, F * D // PER_COL], U16)
        pos_sb = [sb("pos%d_sb" % r, [P, T // PER_COL], U16) for r in range(2)]
        xs = sb("xs", [P, T], U8)
        xw = [sb("xw%d" % s, [P, T], I32) for s in range(PASSES)]
        ww = [sb("ww%d" % u, [P, E, 2 * N], U8) for u in range(2)]
        ws = sb("ws", [P, E * PASSES, N], U8)
        es = [sb("es%d" % s, [P, SLOTS], U8) for s in range(PASSES)]
        scattered = sb("scattered", [P, T], F32)
        pieces = {(f, s): (2 if (f, s) in HALVED else 1) for f in range(F) for s in range(PASSES)}
        wa_raw = {
            (f, s): [sb("wa_raw%d%d%d" % (f, s, u), [P, PACK, H // n], F32, tag="wa_raw%d%d%d" % (f, s, u)) for u in range(n)] for (f, s), n in pieces.items()
        }
        wb_raw = [sb("wb_raw%d" % u, [P, F // 2, PACK, N], F32, tag="wb_raw%d" % u) for u in range(2)]
        g_sb = [[sb("g%d%d" % (h, r), [P, T // 2], F32) for r in range(2)] for h in range(2)]
        g_rows = sb("g_rows", [P, P], F32, tag="g_rows")
        g_cols = sb("g_cols", [P, 2 * T // P], F32)
        ident = sb("ident", [P, P], F32)
        q_sb = sb("q_sb", [P, F * D], F32)

        nc.gpsimd.memset(xs[:].bitcast(I32), 0)
        nc.vector.memset(ws[:].rearrange("p a n -> p (a n)").bitcast(I32), 0)
        nc.vector.memset(es[1][:].bitcast(I32), 0)
        nc.gpsimd.memset(g_rows[:], 0.0)
        make_identity(nc, ident[:])
        nc.gpsimd.memset(scattered[:], 0.0)

        def load_wa(f, s, only=None):
            width = H // pieces[f, s]
            for u, raw in enumerate(wa_raw[f, s]):
                if only is not None and u != only:
                    continue
                src = wa[f, s * PASS : (s + 1) * PASS, u * width : (u + 1) * width]
                nc.sync.dma_start(raw[:], src.rearrange("(p j) c -> p j c", j=PACK))

        def load_wb(u):
            half = wb[u * F // 2 : (u + 1) * F // 2]
            nc.sync.dma_start(wb_raw[u][:].rearrange("p f j n -> p f (j n)"), half.rearrange("f (p j) n -> p f (j n)", j=PACK))

        def load_xw(s):
            nc.sync.dma_start(xw[s][:], x_words[s].rearrange("p t d -> p (t d)").bitcast(I32))

        as_sb = sb("as_sb", [P, F * D], U8)
        aw = [sb("aw%d" % s, [P, F * D], U32) for s in range(PASSES)]

        nc.sync.dma_start(offs_sb[:], offs)
        for q in range(4):
            nc.sync.dma_start(xs[32 * q : 32 * q + 8, :].bitcast(I32), x_scales[:, 4 * q : 4 * q + 4, :].bitcast(I32))
        nc.sync.dma_start(offs2_sb[:], offs2)
        load_wa(0, 0)
        load_wa(0, 1)
        nc.sync.dma_start(g_rows[0 : 2 * T // P, :], gate[:, 0, :].rearrange("r (b p) -> r b p", p=P))
        load_xw(0)
        load_xw(1)
        for r in range(4):
            nc.sync.dma_start(
                ws[r:P:32, :, :].bitcast(I32),
                w_scales[:, :, r:16:4, :].rearrange("e s b n -> b (e s) n").bitcast(I32),
            )
        load_wa(1, 0)
        for a, b in ((0, 768), (768, 1536), (1536, 2048)):
            nc.vector.tensor_copy(es[0][:, a:b], xs[:].indirect(offs_sb[:, a // PER_COL : b // PER_COL]))
        nc.vector.tensor_copy(as_sb[:], xs[:].indirect(offs2_sb[:]))
        for s in range(PASSES):
            nc.vector.tensor_copy(aw[s][:], xw[s][:].bitcast(U32).indirect(offs2_sb[:]))
        nc.sync.dma_start(pos_sb[0][:], pos1)
        nc.sync.dma_start(pos_sb[1][:], pos2)
        for r in range(4):
            nc.sync.dma_start(es[1][r:P:32, :].bitcast(I32), es[0][4 + r : P : 32, :].bitcast(I32))
        for u in range(2):
            half = w_words[u * E // 2 : (u + 1) * E // 2]
            nc.sync.dma_start(ww[u][:].bitcast(I32), half.rearrange("e s p n -> p (e s) n").bitcast(I32))
        load_wa(1, 1)
        load_wa(2, 0)
        load_wa(2, 1)
        load_wa(3, 0)
        load_wa(3, 1)
        load_wb(0)
        nc.sync.dma_start(q_sb[:], gate2)
        load_wb(1)

        wa_q = [[sb("wa_q%d%d" % (f, s), [P, H], U32) for s in range(PASSES)] for f in range(F)]
        wa_s = [[sb("wa_s%d%d" % (f, s), [P, H], U8) for s in range(PASSES)] for f in range(F)]
        wb_q = [sb("wb_q%d" % u, [P, F * N // 2], U32) for u in range(2)]
        wb_s = [sb("wb_s%d" % u, [P, F * N // 2], U8) for u in range(2)]
        y_sb = sb("y_sb", [P, SLOTS], F32)
        y_ps = {}
        h_ps = [psum.tile([P, H], F32, name="h_ps%d" % u) for u in range(2)]
        turn_ps = psum.tile([P, 2, D], F32, name="turn_ps")

        def prep_wa(f, s):
            wa_bf = sb("wa_bf%d%d" % (f, s), [P, H, PACK], BF16, tag="stage%d" % (f * PASSES + s))
            width = H // pieces[f, s]
            for u, raw in enumerate(wa_raw[f, s]):
                share = ON_VECTOR.get((f, s, u), 0)
                for cast, a, b in ((nc.scalar.copy, 0, width - share), (nc.vector.tensor_copy, width - share, width)):
                    if b > a:
                        cast(
                            wa_bf[:, u * width + a : u * width + b, :].rearrange("p (c i) j -> p c j i", i=PACK),
                            raw[:, :, a:b].rearrange("p j (c i) -> p c j i", i=PACK),
                        )
            width = H // (LAST_SPLIT if (f, s) == (F - 1, PASSES - 1) else 1)
            for c0 in range(0, H, width):
                cols = slice(c0, c0 + width)
                nc.vector.quantize_mx(
                    out=wa_q[f][s][:, cols].bitcast(FP8X4),
                    scales=wa_s[f][s][:, cols],
                    in_=wa_bf[:, cols, :].rearrange("p c j -> p (c j)"),
                )

        def prep_wb(u, cast):
            wb_bf = sb("wb_bf%d" % u, [P, F // 2, N, PACK], BF16, tag="wb_bf%d" % u)
            cast(
                wb_bf[:].rearrange("p f (c i) j -> p f c j i", i=PACK),
                wb_raw[u][:].rearrange("p f j (c i) -> p f c j i", i=PACK),
            )
            nc.vector.quantize_mx(out=wb_q[u][:].bitcast(FP8X4), scales=wb_s[u][:], in_=wb_bf[:].rearrange("p f n j -> p (f n j)"))

        def gate_columns():
            nc.tensor.transpose(turn_ps[:, 0, :], g_rows[:], ident[:])
            nc.scalar.copy(g_cols[:], turn_ps[:, 0, 0 : 2 * T // P])

        def spread_gate(h, r):
            g_ps = psum.tile([P, T // 2], F32, name="g_ps%d%d" % (h, r), tag="bank%d" % (2 * h + r))
            for b in range(T // 2 // P):
                j = (r * T + h * T // 2) // P + b
                nc.tensor.transpose(g_ps[:, b * P : (b + 1) * P], g_cols[:, j : j + 1].to_broadcast([P, P]), ident[:])
            nc.scalar.copy(g_sb[h][r][:], g_ps[:])

        def experts(c, tag):
            ew = sb("ew%d" % c, [P, PASSES, BANK], U32, tag=tag)
            for s in range(PASSES):
                picks = offs_sb[:, c * BANK // PER_COL : (c + 1) * BANK // PER_COL]
                nc.vector.tensor_copy(ew[:, s, :], xw[s][:].bitcast(U32).indirect(picks))
            y_ps[c] = psum.tile([P, BANK], F32, name="y_ps%d" % c, tag="bank%d" % c)
            for u in range(BANK // C):
                e = c * (BANK // C) + u
                cols = slice(u * C, (u + 1) * C)
                for s in range(PASSES):
                    nc.tensor.matmul_mx(
                        out=y_ps[c][:, cols],
                        lhsT=ww[2 * e // E][:, (e * PASSES + s) % E, :].bitcast(FP4X4),
                        lhsT_scale=ws[:, e * PASSES + s, :],
                        rhs=ew[:, s, cols].bitcast(FP8X4),
                        rhs_scale=es[s][:, e * C : (e + 1) * C],
                        start=(s == 0),
                        stop=(s == PASSES - 1),
                    )

        def y_out(c):
            if c == CHUNKS - 1:
                nc.vector.tensor_copy(y_sb[:, c * BANK : (c + 1) * BANK], y_ps[c][:])
            else:
                nc.scalar.copy(y_sb[:, c * BANK : (c + 1) * BANK], y_ps[c][:])

        h_q = [sb("h_q%d" % f, [P, D], U32) for f in range(F)]
        h_s = [sb("h_s%d" % f, [P, D], U8) for f in range(F)]

        def adapter_up(f, silu_tag="", turn_tag=None):
            slots = slice(f * D, (f + 1) * D)
            turns = range(PASSES) if f == F - 1 else range(PASSES - 1, -1, -1)
            h_rows = sb("h_rows%d" % f, [P, H], BF16, tag=silu_tag)
            width = H // (LAST_SPLIT if f == F - 1 else 1)
            for c0 in range(0, H, width):
                cols = slice(c0, c0 + width)
                bank = h_ps[(f + c0 // width) % 2]
                for s in turns:
                    nc.tensor.matmul_mx(
                        out=bank[:, cols],
                        lhsT=aw[s][:, slots].bitcast(FP8X4),
                        lhsT_scale=as_sb[4 * s : P, slots],
                        rhs=wa_q[f][s][:, cols].bitcast(FP8X4),
                        rhs_scale=wa_s[f][s][:, cols],
                        start=(s == turns[0]),
                        stop=(s == turns[-1]),
                    )
                nc.scalar.activation(h_rows[:, cols], bank[:, cols], SILU)
            pairs = h_rows[:].bitcast(F32)
            for u in range(2):
                nc.tensor.transpose(turn_ps[:, u, :], pairs[:, u : H // 2 : 2], ident[:])
            h_bf = sb("h_bf%d" % f, [P, D, PACK], BF16, tag=turn_tag or "h_bf%d" % f)
            nc.scalar.copy(
                h_bf[:].rearrange("p m t -> p (m t)").bitcast(F32).rearrange("p (m u) -> p m u", u=2),
                turn_ps[:].rearrange("p u m -> p m u"),
            )
            nc.vector.quantize_mx(out=h_q[f][:].bitcast(FP8X4), scales=h_s[f][:], in_=h_bf[:].rearrange("p m t -> p (m t)"))

        def adapter_down(f, tag=""):
            slots = slice(f * D, (f + 1) * D)
            z_ps = psum.tile([P, D], F32, name="z_ps%d" % f, tag="bank%d" % f)
            nc.tensor.matmul_mx(
                out=z_ps[:],
                lhsT=wb_q[f // 2][:, f % 2 * N : (f % 2 + 1) * N].bitcast(FP8X4),
                lhsT_scale=wb_s[f // 2][:, f % 2 * N : (f % 2 + 1) * N],
                rhs=h_q[f][:].bitcast(FP8X4),
                rhs_scale=h_s[f][:],
                start=True,
                stop=True,
            )
            z_sb = sb("z_sb%d" % f, [P, D], F32, tag=tag)
            nc.scalar.copy(z_sb[:], z_ps[:])
            nc.vector.tensor_tensor(
                scattered[:].indirect(offs2_sb[:, f * D // PER_COL : (f + 1) * D // PER_COL]), z_sb[:], q_sb[:, slots], MULT
            )

        HALF = T // 2
        o_sb = {}

        parts = {}

        def fetch(h, r, tag=""):
            parts[h, r] = sb("part%d%d" % (h, r), [P, HALF], F32, tag=tag)
            nc.vector.tensor_tensor(
                parts[h, r][:],
                y_sb[:].indirect(pos_sb[r][:, h * HALF // PER_COL : (h + 1) * HALF // PER_COL]),
                g_sb[h][r][:],
                MULT,
            )

        def combine(h, tag=""):
            o_sb[h] = sb("o_sb%d" % h, [P, HALF], F32, tag=tag)
            nc.vector.tensor_tensor(o_sb[h][:], parts[h, 0][:], parts[h, 1][:], ADD)

        prep_wa(0, 0)
        prep_wa(0, 1)
        gate_columns()
        for h in range(2):
            for r in range(2):
                spread_gate(h, r)
        experts(0, "stage1")
        experts(1, "wa_raw010")
        prep_wa(1, 0)
        adapter_up(0, "wa_raw100")
        experts(2, "stage2")
        experts(3, "g_rows")
        y_out(0)
        y_out(1)
        y_out(2)
        y_out(3)
        fetch(0, 0)
        fetch(0, 1)
        prep_wa(1, 1)
        combine(0, "stage3")
        fetch(1, 0, "wa_raw110")
        prep_wa(2, 0)
        adapter_up(1, "wa_raw200")
        prep_wa(2, 1)
        fetch(1, 1, "stage4")
        prep_wa(3, 0)
        prep_wa(3, 1)
        adapter_up(2, "wa_raw300", "wa_raw310")
        adapter_up(3)
        combine(1, "stage7")
        prep_wb(0, nc.scalar.copy)
        prep_wb(1, nc.vector.tensor_copy)
        adapter_down(0)
        adapter_down(1)
        adapter_down(2)
        adapter_down(3)
        for h in range(2):
            toks = slice(h * HALF, (h + 1) * HALF)
            res = sb("res%d" % h, [P, HALF], F32)
            nc.vector.tensor_tensor(res[:], o_sb[h][:], scattered[:, toks], ADD)
            nc.sync.dma_start(out[:, toks], res[:])
